import numpy as np
import ml_dtypes


def mxq(x, axis, fmt="e4m3"):
    dtype, down = {"e4m3": (ml_dtypes.float8_e4m3fn, 7), "e5m2": (ml_dtypes.float8_e5m2, 14)}[fmt]
    v = np.moveaxis(np.asarray(x, np.float32).astype(ml_dtypes.bfloat16).astype(np.float64), axis, -1)
    blocks = v.reshape(v.shape[:-1] + (-1, 32))
    amax = np.abs(blocks).max(-1, keepdims=True)
    byte = np.maximum(np.where(amax > 0, np.frexp(amax)[1] - 1 + 127, 0) - down, 1)
    scale = np.exp2(byte - 127.0)
    codes = (blocks / scale).astype(np.float32).astype(dtype).astype(np.float64)
    return np.moveaxis((codes * scale).reshape(v.shape), -1, axis)


WIDE = False


def mx_kscale(k):
    if not WIDE:
        return np.ones(k)
    levels = np.array([10, -10, 5, -5, 0])
    if k % 512:
        return np.exp2(np.random.permutation(np.resize(levels, k // 32))).repeat(32)
    a = np.empty((k // 512, 16))
    for p in range(k // 512):
        a[p, :8] = np.random.permutation(np.resize(levels, 8))
        for g in range(8):
            far = levels[np.abs(levels - a[p, g]) >= 10]
            a[p, g + 8] = far[np.random.randint(len(far))]
    return np.exp2(a.ravel()).repeat(32)


def f64(x):
    return np.asarray(x).astype(np.float64)


E2M1 = np.array([0.0, 0.5, 1.0, 1.5, 2.0, 3.0, 4.0, 6.0, -0.0, -0.5, -1.0, -1.5, -2.0, -3.0, -4.0, -6.0])


def pack_weight(w, fmt):
    k, n = w.shape
    w = f64(np.asarray(w, np.float32).astype(ml_dtypes.bfloat16)).reshape(k // 32, 32, n)
    amax = np.abs(w).max(1)
    if fmt == "e4m3":
        byte = np.frexp(amax)[1] - 1 + 127 - 7
    else:
        mant, ex = np.frexp(amax / 6.0)
        byte = np.where(mant > 0.5, ex, ex - 1) + 127
    byte = np.clip(np.where(amax > 0, byte, 1), 1, 254)
    scaled = (w * np.exp2(127.0 - byte)[:, None, :]).reshape(k, n).astype(np.float32)
    by_word = np.ascontiguousarray(scaled.reshape(k // 512, 128, 4, n).transpose(0, 1, 3, 2))
    if fmt == "e4m3":
        words = by_word.astype(ml_dtypes.float8_e4m3fn).view(np.uint8)
    else:
        c = by_word.astype(ml_dtypes.float4_e2m1fn).view(np.uint8) & 0xF
        words = (c[..., 0::2] | (c[..., 1::2] << 4)).reshape(k // 512, 128, 2 * n)
    return np.ascontiguousarray(words), np.ascontiguousarray(byte.astype(np.uint8).reshape(k // 512, 16, n))


def unpack_weight(words, scales, fmt):
    g, _, n = scales.shape
    words = np.ascontiguousarray(words).reshape(g, 128, n, -1)
    if fmt == "e4m3":
        vals = words.view(ml_dtypes.float8_e4m3fn).astype(np.float64)
    else:
        nib = np.empty((g, 128, n, 4), np.uint8)
        nib[..., 0::2] = words & 0xF
        nib[..., 1::2] = words >> 4
        vals = E2M1[nib]
    vals = vals * np.repeat(np.exp2(scales.astype(np.float64) - 127.0), 8, axis=1)[..., None]
    return vals.transpose(0, 1, 3, 2).reshape(g * 512, n)


K, L, M, T, B, N = 1024, 512, 512, 1024, 256, 512


def setup_inputs():
    n = np.random.standard_normal
    fk = mx_kscale(K)
    fl = mx_kscale(L)
    fm = mx_kscale(M)
    xtp = pack_weight(n((K, T)) / fk[:, None], "e4m3")
    xqp = pack_weight(n((L, T)) / fl[:, None], "e2m1")
    wqp = pack_weight(n((L, N)) * 1 / np.sqrt(L) * fl[:, None], "e4m3")
    xgp = pack_weight(n((M, B)) / fm[:, None], "e4m3")
    return {
        "xt_words": xtp[0],
        "xt_scales": xtp[1],
        "wa": (n((K, N)) * 1 / np.sqrt(K) * fk[:, None]).astype(np.float32),
        "xq_words": xqp[0],
        "xq_scales": xqp[1],
        "wq_words": wqp[0],
        "wq_scales": wqp[1],
        "xg_words": xgp[0],
        "xg_scales": xgp[1],
        "wg": (n((M, N)) * 1 / np.sqrt(M) * fm[:, None]).astype(np.float32),
    }


def reference(xt_words, xt_scales, wa, xq_words, xq_scales, wq_words, wq_scales, xg_words, xg_scales, wg):
    xtu = unpack_weight(xt_words, xt_scales, "e4m3")
    xqu = unpack_weight(xq_words, xq_scales, "e2m1")
    wqu = unpack_weight(wq_words, wq_scales, "e4m3")
    xgu = unpack_weight(xg_words, xg_scales, "e4m3")
    waq = mxq(f64(wa), 0, "e4m3")
    z = waq.T @ xtu + wqu.T @ xqu
    mz = z.reshape(N, B, T // B).mean(axis=2)
    wgq = mxq(f64(wg), 0, "e4m3")
    g = wgq.T @ xgu
    s = mz + g
    sr = np.repeat(s, T // B, axis=1)
    y = 0.4 * z + np.maximum(sr, 0.0)
    return y

@@ -1,0 +1,353 @@
+from contextlib import ExitStack
+
+import concourse.mybir as mybir
+
+K, L, M, T, B, N = 1024, 512, 512, 1024, 256, 512
+FLOPS = 2 * N * (K * T + L * T + M * B)
+
+F32 = mybir.dt.float32
+BF16 = mybir.dt.bfloat16
+I32 = mybir.dt.int32
+U32 = mybir.dt.uint32
+U8 = mybir.dt.uint8
+FP8X4 = mybir.dt.float8_e4m3fn_x4
+FP4X4 = mybir.dt.float4_e2m1fn_x4
+ALU = mybir.AluOpType
+ACT = mybir.ActivationFunctionType
+
+P = 128
+PACK = 4
+K_PASS = P * PACK
+HALF = 512
+GROUP = T // B
+HALF_GROUPS = HALF // GROUP
+
+
+def tile_mix_sum_shared_by_neighbours_kernel(
+    tc, xt_words, xt_scales, wa, xq_words, xq_scales, wq_words, wq_scales, xg_words, xg_scales, wg, out
+):
+    nc = tc.nc
+    with ExitStack() as ctx:
+        keep = ctx.enter_context(tc.tile_pool(name="keep", bufs=1))
+        zpool = ctx.enter_context(tc.psum_pool(name="zpool", bufs=6))
+        gpool = ctx.enter_context(tc.psum_pool(name="gpool", bufs=2))
+        ctx.enter_context(tc.manual_schedule())
+
+        def sb(name, shape, dtype):
+            return keep.tile(shape, dtype, name=name, align_bytes=64)
+
+        xt_plane = sb("xt_plane", [P, T], U8)
+        wq_plane = sb("wq_plane", [P, N], U8)
+        xq_plane = sb("xq_plane", [P, T], U8)
+        nc.vector.memset(xt_plane[:].bitcast(I32), 0)
+        nc.vector.memset(wq_plane[:].bitcast(I32), 0)
+        nc.gpsimd.memset(xq_plane[:].bitcast(I32), 0)
+
+        def load_scales(engine, plane, first_row, cols, scales, quads=range(4)):
+            passes = scales.shape[0]
+            for q in quads:
+                rows = slice(32 * q + first_row, 32 * q + first_row + 4 * passes)
+                src = scales[:, 4 * q : 4 * q + 4, :] if passes > 1 else scales[0, 4 * q : 4 * q + 4, :]
+                engine.dma_start(out=plane[rows, cols].bitcast(I32), in_=src.bitcast(I32))
+
+
+        raw = {}
+
+        def load_weight(name, w, z, i0, i1):
+            t = sb("raw_%s%d_%d" % (name, z, i0), [P, PACK, (i1 - i0) * P], F32)
+            rows = w[z * K_PASS : (z + 1) * K_PASS, :].rearrange("(p j) n -> p j n", j=PACK)
+            nc.sync.dma_start(out=t[:], in_=rows[:, :, i0 * P : i1 * P])
+            for i in range(i0, i1):
+                raw[name, z, i] = t[:, :, (i - i0) * P : (i - i0 + 1) * P]
+
+        xt_sb = {}
+
+        def load_xt(h):
+            t = sb("xt_sb%d" % h, [P, 2, HALF], U32)
+            src = xt_words.rearrange("z p t r -> p z (t r)")[:, :, h * HALF * 4 : (h + 1) * HALF * 4]
+            nc.sync.dma_start(out=t[:].bitcast(I32), in_=src.bitcast(I32))
+            xt_sb[h] = t
+
+        wq_sb = sb("wq_sb", [P, N], U32)
+        xq_sb = sb("xq_sb", [P, 2 * T], U8)
+        xg_sb = sb("xg_sb", [P, B], U32)
+
+        def load_wq():
+            nc.sync.dma_start(out=wq_sb[:].bitcast(I32), in_=wq_words[0].rearrange("p n r -> p (n r)").bitcast(I32))
+
+        def load_xq():
+            nc.sync.dma_start(out=xq_sb[:].bitcast(I32), in_=xq_words[0].bitcast(I32))
+
+        def load_xg():
+            nc.sync.dma_start(out=xg_sb[:].bitcast(I32), in_=xg_words[0].rearrange("p b r -> p (b r)").bitcast(I32))
+
+        def sc_xt(engine, quads):
+            load_scales(engine, xt_plane, 4, slice(0, T), xt_scales, quads)
+
+        def sc_wq(engine, quads):
+            load_scales(engine, wq_plane, 0, slice(0, N), wq_scales, quads)
+
+        def sc_xq(engine, quads):
+            load_scales(engine, xq_plane, 0, slice(0, T), xq_scales, quads)
+
+        def sc_xg(engine, quads):
+            load_scales(engine, xt_plane, 12, slice(HALF, HALF + B), xg_scales, quads)
+
+        sc_xq(nc.gpsimd, (0, 1, 2, 3,))
+        sc_xg(nc.gpsimd, (0, 1, 2, 3,))
+        load_weight("a", wa, 0, 0, 2)
+        sc_xt(nc.sync, (0, 1,))
+        load_weight("a", wa, 1, 0, 2)
+        sc_xt(nc.sync, (2, 3,))
+        load_xt(0)
+        sc_wq(nc.sync, (0, 1,))
+        load_wq()
+        sc_wq(nc.sync, (2, 3,))
+        load_xq()
+        load_weight("g", wg, 0, 0, 2)
+        load_xg()
+        load_weight("a", wa, 0, 2, 3)
+        load_weight("a", wa, 1, 2, 3)
+        load_xt(1)
+        load_weight("g", wg, 0, 2, 3)
+        load_weight("a", wa, 0, 3, 4)
+        load_weight("a", wa, 1, 3, 4)
+        load_weight("g", wg, 0, 3, 4)
+
+        staged, codes, planes = {}, {}, {}
+        for name, count in (("a", 4), ("g", 2)):
+            for i in range(count):
+                staged[name, i] = sb("staged_%s%d" % (name, i), [P, 2 * K_PASS], BF16)
+                codes[name, i] = sb("codes_%s%d" % (name, i), [P, 2 * P], U32)
+                planes[name, i] = sb("planes_%s%d" % (name, i), [P, 2 * P], U8)
+
+        def cast(engine, name, z, i):
+            key, slot = ((name, i), z) if name == "a" else ((name, i // 2), i % 2)
+            dst = staged[key][:, slot * K_PASS : (slot + 1) * K_PASS]
+            src = raw[name, z, i]
+            if engine == "gpsimd":
+                nc.gpsimd.tensor_scalar(
+                    out=dst.rearrange("p (c j) -> p c j", j=PACK),
+                    in0=src.rearrange("p j c -> p c j"),
+                    scalar1=1.0,
+                    scalar2=0.0,
+                    op0=ALU.mult,
+                    op1=ALU.add,
+                )
+                return
+            dst = dst.rearrange("p (c u j) -> p c j u", u=4, j=PACK)
+            src = src.rearrange("p j (c u) -> p c j u", u=4)
+            if engine == "vector":
+                nc.vector.tensor_copy(out=dst, in_=src)
+            else:
+                nc.scalar.copy(out=dst, in_=src)
+
+        def quantise(name, i, z0=0, z1=2):
+            nc.vector.quantize_mx(
+                out=codes[name, i][:, z0 * P : z1 * P].bitcast(FP8X4),
+                scales=planes[name, i][:, z0 * P : z1 * P],
+                in_=staged[name, i][:, z0 * K_PASS : z1 * K_PASS],
+            )
+        zb, gb = {}, {}
+
+        def z_tile(i, h):
+            if (i, h) not in zb:
+                zb[i, h] = zpool.tile([P, HALF], F32, name="z")
+            return zb[i, h]
+
+        def pass_q(i, h, start, stop):
+            nc.tensor.matmul_mx(
+                out=z_tile(i, h)[:],
+                lhsT=wq_sb[:, i * P : (i + 1) * P].bitcast(FP8X4),
+                lhsT_scale=wq_plane[:, i * P : (i + 1) * P],
+                rhs=xq_sb[:, 2 * h * HALF : 2 * (h + 1) * HALF].bitcast(FP4X4),
+                rhs_scale=xq_plane[:, h * HALF : (h + 1) * HALF],
+                start=start,
+                stop=stop,
+            )
+
+        def pass_t(i, h, z, start, stop):
+            nc.tensor.matmul_mx(
+                out=z_tile(i, h)[:],
+                lhsT=codes["a", i][:, z * P : (z + 1) * P].bitcast(FP8X4),
+                lhsT_scale=planes["a", i][:, z * P : (z + 1) * P],
+                rhs=xt_sb[h][:, z, :].bitcast(FP8X4),
+                rhs_scale=xt_plane[4 + 4 * z :, h * HALF : (h + 1) * HALF],
+                start=start,
+                stop=stop,
+            )
+
+        def passes_t(i, h):
+            pass_t(i, h, 0, False, False)
+            pass_t(i, h, 1, False, True)
+
+        def pass_g(i):
+            gb[i] = gpool.tile([P, B], F32, name="g")
+            slot = slice((i % 2) * P, (i % 2 + 1) * P)
+            nc.tensor.matmul_mx(
+                out=gb[i][:],
+                lhsT=codes["g", i // 2][:, slot].bitcast(FP8X4),
+                lhsT_scale=planes["g", i // 2][:, slot],
+                rhs=xg_sb[:].bitcast(FP8X4),
+                rhs_scale=xt_plane[12:, HALF : HALF + B],
+                start=True,
+                stop=True,
+            )
+
+        sums, pre, shared, scaled, res = {}, {}, {}, {}, {}
+        for i in range(4):
+            sums[i] = sb("sums%d" % i, [P, B], F32)
+            pre[i] = sb("pre%d" % i, [P, B], F32)
+            shared[i] = sb("shared%d" % i, [P, B], F32)
+
+        def groups(h0, h1):
+            return slice(h0 * HALF_GROUPS, h1 * HALF_GROUPS)
+
+        def group_sum(i, h):
+            nc.vector.tensor_reduce(
+                out=sums[i][:, groups(h, h + 1)],
+                in_=zb[i, h][:].rearrange("p (b j) -> p b j", j=GROUP),
+                axis=mybir.AxisListType.X,
+                op=ALU.add,
+            )
+
+        def add_g(i, h0, h1):
+            nc.vector.scalar_tensor_tensor(
+                out=pre[i][:, groups(h0, h1)],
+                in0=sums[i][:, groups(h0, h1)],
+                scalar=1.0 / GROUP,
+                in1=gb[i][:, groups(h0, h1)],
+                op0=ALU.mult,
+                op1=ALU.add,
+            )
+
+        def relu(i, h0, h1):
+            nc.scalar.activation(out=shared[i][:, groups(h0, h1)], in_=pre[i][:, groups(h0, h1)], func=ACT.Relu)
+
+        def spread(i, h, c0, c1):
+            b0, b1 = h * HALF_GROUPS + c0 // GROUP, h * HALF_GROUPS + c1 // GROUP
+            return shared[i][:, b0:b1].unsqueeze(2).to_broadcast([P, b1 - b0, GROUP])
+
+        def store(i, h, c0, c1):
+            nc.sync.dma_start(out=out[i * P : (i + 1) * P, h * HALF + c0 : h * HALF + c1], in_=res[i, h, c0][:])
+
+        def finish_vector(i, h, c0=0, c1=HALF):
+            res[i, h, c0] = sb("res%d_%d_%d" % (i, h, c0), [P, c1 - c0], F32)
+            nc.vector.scalar_tensor_tensor(
+                out=res[i, h, c0][:].rearrange("p (b j) -> p b j", j=GROUP),
+                in0=zb[i, h][:, c0:c1].rearrange("p (b j) -> p b j", j=GROUP),
+                scalar=0.4,
+                in1=spread(i, h, c0, c1),
+                op0=ALU.mult,
+                op1=ALU.add,
+            )
+
+        def finish_fused(i, h, c0=0, c1=HALF):
+            res[i, h, c0] = sb("res%d_%d_%d" % (i, h, c0), [P, c1 - c0], F32)
+            b0, b1 = h * HALF_GROUPS + c0 // GROUP, h * HALF_GROUPS + c1 // GROUP
+            nc.vector.scalar_tensor_tensor(
+                out=res[i, h, c0][:].rearrange("p (b j) -> p b j", j=GROUP),
+                in0=pre[i][:, b0:b1].unsqueeze(2).to_broadcast([P, b1 - b0, GROUP]),
+                scalar=0.0,
+                in1=scaled[i, h, c0][:].rearrange("p (b j) -> p b j", j=GROUP),
+                op0=ALU.max,
+                op1=ALU.add,
+            )
+
+        def scale_out(i, h, c0=0, c1=HALF):
+            scaled[i, h, c0] = sb("scaled%d_%d_%d" % (i, h, c0), [P, c1 - c0], F32)
+            nc.scalar.activation(out=scaled[i, h, c0][:], in_=zb[i, h][:, c0:c1], func=ACT.Copy, scale=0.4)
+
+        def finish_gpsimd(i, h, c0=0, c1=HALF):
+            res[i, h, c0] = sb("res%d_%d_%d" % (i, h, c0), [P, c1 - c0], F32)
+            nc.gpsimd.tensor_tensor(
+                out=res[i, h, c0][:].rearrange("p (b j) -> p b j", j=GROUP),
+                in0=scaled[i, h, c0][:].rearrange("p (b j) -> p b j", j=GROUP),
+                in1=spread(i, h, c0, c1),
+                op=ALU.add,
+            )
+
+        cast("vector", "a", 0, 0)
+        cast("scalar", "a", 0, 1)
+        cast("vector", "a", 1, 0)
+        cast("scalar", "a", 1, 1)
+        quantise("a", 0)
+        quantise("a", 1)
+        pass_t(0, 0, 0, True, False)
+        pass_t(0, 0, 1, False, False)
+        pass_q(0, 0, False, True)
+        pass_t(1, 0, 0, True, False)
+        pass_t(1, 0, 1, False, False)
+        pass_q(1, 0, False, True)
+        pass_q(2, 0, True, False)
+        pass_q(0, 1, True, False)
+        pass_q(1, 1, True, False)
+        pass_q(2, 1, True, False)
+        group_sum(0, 0)
+        cast("vector", "g", 0, 0)
+        cast("scalar", "g", 0, 1)
+        group_sum(1, 0)
+        scale_out(0, 0, 0, 512)
+        quantise("g", 0)
+        pass_g(0)
+        pass_g(1)
+        cast("vector", "a", 0, 2)
+        scale_out(1, 0, 0, 512)
+        cast("vector", "a", 1, 2)
+        add_g(0, 0, 1)
+        add_g(1, 0, 1)
+        relu(0, 0, 1)
+        relu(1, 0, 1)
+        quantise("a", 2)
+        finish_gpsimd(0, 0, 0, 512)
+        store(0, 0, 0, 512)
+        passes_t(0, 1)
+        passes_t(2, 0)
+        passes_t(1, 1)
+        passes_t(2, 1)
+        pass_q(3, 0, True, False)
+        pass_q(3, 1, True, False)
+        cast("scalar", "g", 0, 2)
+        group_sum(0, 1)
+        cast("scalar", "a", 0, 3)
+        group_sum(2, 0)
+        add_g(0, 1, 2)
+        cast("scalar", "a", 1, 3)
+        group_sum(1, 1)
+        quantise("g", 1, 0, 1)
+        pass_g(2)
+        quantise("a", 3)
+        finish_gpsimd(1, 0, 0, 512)
+        store(1, 0, 0, 512)
+        passes_t(3, 0)
+        passes_t(3, 1)
+        relu(0, 1, 2)
+        cast("scalar", "g", 0, 3)
+        add_g(1, 1, 2)
+        add_g(2, 0, 1)
+        group_sum(2, 1)
+        relu(1, 1, 2)
+        relu(2, 0, 1)
+        scale_out(0, 1, 0, 512)
+        finish_vector(1, 1, 0, 512)
+        store(1, 1, 0, 512)
+        quantise("g", 1, 1, 2)
+        pass_g(3)
+        finish_gpsimd(0, 1, 0, 512)
+        store(0, 1, 0, 512)
+        add_g(2, 1, 2)
+        group_sum(3, 0)
+        finish_vector(2, 0, 0, 512)
+        store(2, 0, 0, 512)
+        relu(2, 1, 2)
+        scale_out(2, 1, 0, 512)
+        group_sum(3, 1)
+        finish_gpsimd(2, 1, 0, 512)
+        store(2, 1, 0, 512)
+        add_g(3, 0, 2)
+        scale_out(3, 0, 0, 512)
+        scale_out(3, 1, 0, 512)
+        finish_fused(3, 0, 0, 512)
+        store(3, 0, 0, 512)
+        finish_fused(3, 1, 0, 512)
+        store(3, 1, 0, 512)

@@ -40,8 +40,8 @@ def tile_mix_sum_shared_by_neighbours_kernel(
         wq_plane = sb("wq_plane", [P, N], U8)
         xq_plane = sb("xq_plane", [P, T], U8)
         nc.vector.memset(xt_plane[:].bitcast(I32), 0)
+        nc.vector.memset(xq_plane[:].bitcast(I32), 0)
         nc.vector.memset(wq_plane[:].bitcast(I32), 0)
-        nc.gpsimd.memset(xq_plane[:].bitcast(I32), 0)
 
         def load_scales(engine, plane, first_row, cols, scales, quads=range(4)):
             passes = scales.shape[0]
@@ -93,18 +93,18 @@ def tile_mix_sum_shared_by_neighbours_kernel(
         def sc_xg(engine, quads):
             load_scales(engine, xt_plane, 12, slice(HALF, HALF + B), xg_scales, quads)
 
-        sc_xq(nc.gpsimd, (0, 1, 2, 3,))
         sc_xg(nc.gpsimd, (0, 1, 2, 3,))
         load_weight("a", wa, 0, 0, 2)
-        sc_xt(nc.sync, (0, 1,))
+        sc_xt(nc.sync, (0, 1, 2, 3,))
         load_weight("a", wa, 1, 0, 2)
-        sc_xt(nc.sync, (2, 3,))
+        sc_xq(nc.sync, (0,))
         load_xt(0)
-        sc_wq(nc.sync, (0, 1,))
-        load_wq()
-        sc_wq(nc.sync, (2, 3,))
-        load_xq()
+        sc_xq(nc.sync, (1, 2, 3,))
+        sc_wq(nc.sync, (0,))
         load_weight("g", wg, 0, 0, 2)
+        load_wq()
+        load_xq()
+        sc_wq(nc.sync, (1, 2, 3,))
         load_xg()
         load_weight("a", wa, 0, 2, 3)
         load_weight("a", wa, 1, 2, 3)
@@ -275,78 +275,77 @@ def tile_mix_sum_shared_by_neighbours_kernel(
         quantise("a", 1)
         pass_t(0, 0, 0, True, False)
         pass_t(0, 0, 1, False, False)
-        pass_q(0, 0, False, True)
         pass_t(1, 0, 0, True, False)
         pass_t(1, 0, 1, False, False)
+        cast("vector", "g", 0, 0)
+        cast("scalar", "g", 0, 1)
+        quantise("g", 0)
+        pass_q(0, 0, False, True)
         pass_q(1, 0, False, True)
+        pass_g(0)
+        pass_g(1)
         pass_q(2, 0, True, False)
         pass_q(0, 1, True, False)
         pass_q(1, 1, True, False)
         pass_q(2, 1, True, False)
         group_sum(0, 0)
-        cast("vector", "g", 0, 0)
-        cast("scalar", "g", 0, 1)
+        cast("scalar", "a", 0, 2)
         group_sum(1, 0)
-        scale_out(0, 0, 0, 512)
-        quantise("g", 0)
-        pass_g(0)
-        pass_g(1)
-        cast("vector", "a", 0, 2)
-        scale_out(1, 0, 0, 512)
-        cast("vector", "a", 1, 2)
+        cast("scalar", "a", 1, 2)
         add_g(0, 0, 1)
         add_g(1, 0, 1)
-        relu(0, 0, 1)
-        relu(1, 0, 1)
         quantise("a", 2)
-        finish_gpsimd(0, 0, 0, 512)
-        store(0, 0, 0, 512)
+        relu(0, 0, 1)
+        scale_out(1, 0, 0, 512)
+        relu(1, 0, 1)
+        finish_gpsimd(1, 0, 0, 512)
+        store(1, 0, 0, 512)
         passes_t(0, 1)
         passes_t(2, 0)
         passes_t(1, 1)
         passes_t(2, 1)
+        finish_vector(0, 0, 0, 512)
+        store(0, 0, 0, 512)
         pass_q(3, 0, True, False)
         pass_q(3, 1, True, False)
         cast("scalar", "g", 0, 2)
         group_sum(0, 1)
         cast("scalar", "a", 0, 3)
         group_sum(2, 0)
-        add_g(0, 1, 2)
         cast("scalar", "a", 1, 3)
+        add_g(0, 1, 2)
         group_sum(1, 1)
         quantise("g", 1, 0, 1)
         pass_g(2)
         quantise("a", 3)
-        finish_gpsimd(1, 0, 0, 512)
-        store(1, 0, 0, 512)
         passes_t(3, 0)
         passes_t(3, 1)
         relu(0, 1, 2)
+        scale_out(0, 1, 0, 512)
+        finish_gpsimd(0, 1, 0, 512)
+        store(0, 1, 0, 512)
         cast("scalar", "g", 0, 3)
         add_g(1, 1, 2)
         add_g(2, 0, 1)
-        group_sum(2, 1)
         relu(1, 1, 2)
         relu(2, 0, 1)
-        scale_out(0, 1, 0, 512)
-        finish_vector(1, 1, 0, 512)
-        store(1, 1, 0, 512)
+        scale_out(2, 0, 0, 512)
+        group_sum(2, 1)
+        group_sum(3, 0)
         quantise("g", 1, 1, 2)
         pass_g(3)
-        finish_gpsimd(0, 1, 0, 512)
-        store(0, 1, 0, 512)
-        add_g(2, 1, 2)
-        group_sum(3, 0)
-        finish_vector(2, 0, 0, 512)
+        finish_gpsimd(2, 0, 0, 512)
         store(2, 0, 0, 512)
+        add_g(2, 1, 2)
+        finish_vector(1, 1, 0, 512)
+        store(1, 1, 0, 512)
         relu(2, 1, 2)
-        scale_out(2, 1, 0, 512)
+        scale_out(3, 0, 0, 512)
         group_sum(3, 1)
-        finish_gpsimd(2, 1, 0, 512)
+        scale_out(3, 1, 0, 512)
+        finish_vector(2, 1, 0, 512)
         store(2, 1, 0, 512)
         add_g(3, 0, 2)
-        scale_out(3, 0, 0, 512)
-        scale_out(3, 1, 0, 512)
         finish_fused(3, 0, 0, 512)
         store(3, 0, 0, 512)
         finish_fused(3, 1, 0, 512)

@@ -21,6 +21,7 @@ K_PASS = P * PACK
 HALF = 512
 GROUP = T // B
 HALF_GROUPS = HALF // GROUP
+BANK = {(1, 0): 1, (1, 1): 5, (2, 0): 2, (2, 1): 0, (3, 0): 3, (3, 1): 1, (0, 0): 0, (0, 1): 4}
 
 
 def tile_mix_sum_shared_by_neighbours_kernel(
@@ -29,7 +30,7 @@ def tile_mix_sum_shared_by_neighbours_kernel(
     nc = tc.nc
     with ExitStack() as ctx:
         keep = ctx.enter_context(tc.tile_pool(name="keep", bufs=1))
-        zpool = ctx.enter_context(tc.psum_pool(name="zpool", bufs=6))
+        zpool = ctx.enter_context(tc.psum_pool(name="zpool", bufs=1))
         gpool = ctx.enter_context(tc.psum_pool(name="gpool", bufs=2))
         ctx.enter_context(tc.manual_schedule())
 
@@ -93,26 +94,19 @@ def tile_mix_sum_shared_by_neighbours_kernel(
         def sc_xg(engine, quads):
             load_scales(engine, xt_plane, 12, slice(HALF, HALF + B), xg_scales, quads)
 
-        sc_xg(nc.gpsimd, (0, 1, 2, 3,))
-        load_weight("a", wa, 0, 0, 2)
+        sc_xq(nc.gpsimd, (0, 1, 2, 3,))
+        load_weight("a", wa, 0, 0, 4)
         sc_xt(nc.sync, (0, 1, 2, 3,))
-        load_weight("a", wa, 1, 0, 2)
-        sc_xq(nc.sync, (0,))
         load_xt(0)
-        sc_xq(nc.sync, (1, 2, 3,))
+        load_weight("a", wa, 1, 0, 4)
         sc_wq(nc.sync, (0,))
-        load_weight("g", wg, 0, 0, 2)
         load_wq()
         load_xq()
         sc_wq(nc.sync, (1, 2, 3,))
+        load_weight("g", wg, 0, 0, 4)
         load_xg()
-        load_weight("a", wa, 0, 2, 3)
-        load_weight("a", wa, 1, 2, 3)
+        sc_xg(nc.sync, (0, 1, 2, 3,))
         load_xt(1)
-        load_weight("g", wg, 0, 2, 3)
-        load_weight("a", wa, 0, 3, 4)
-        load_weight("a", wa, 1, 3, 4)
-        load_weight("g", wg, 0, 3, 4)
 
         staged, codes, planes = {}, {}, {}
         for name, count in (("a", 4), ("g", 2)):
@@ -152,7 +146,7 @@ def tile_mix_sum_shared_by_neighbours_kernel(
 
         def z_tile(i, h):
             if (i, h) not in zb:
-                zb[i, h] = zpool.tile([P, HALF], F32, name="z")
+                zb[i, h] = zpool.tile([P, HALF], F32, name="z%d%d" % (i, h), tag="bank%d" % BANK[i, h])
             return zb[i, h]
 
         def pass_q(i, h, start, stop):
@@ -181,11 +175,12 @@ def tile_mix_sum_shared_by_neighbours_kernel(
             pass_t(i, h, 0, False, False)
             pass_t(i, h, 1, False, True)
 
-        def pass_g(i):
-            gb[i] = gpool.tile([P, B], F32, name="g")
+        def pass_g(i, fresh):
+            if fresh:
+                gb[i // 2] = gpool.tile([P, 2 * B], F32, name="g")
             slot = slice((i % 2) * P, (i % 2 + 1) * P)
             nc.tensor.matmul_mx(
-                out=gb[i][:],
+                out=gb[i // 2][:, (i % 2) * B : (i % 2 + 1) * B],
                 lhsT=codes["g", i // 2][:, slot].bitcast(FP8X4),
                 lhsT_scale=planes["g", i // 2][:, slot],
                 rhs=xg_sb[:].bitcast(FP8X4),
@@ -216,7 +211,7 @@ def tile_mix_sum_shared_by_neighbours_kernel(
                 out=pre[i][:, groups(h0, h1)],
                 in0=sums[i][:, groups(h0, h1)],
                 scalar=1.0 / GROUP,
-                in1=gb[i][:, groups(h0, h1)],
+                in1=gb[i // 2][:, (i % 2) * B : (i % 2 + 1) * B][:, groups(h0, h1)],
                 op0=ALU.mult,
                 op1=ALU.add,
             )
@@ -268,85 +263,92 @@ def tile_mix_sum_shared_by_neighbours_kernel(
             )
 
         cast("vector", "a", 0, 0)
-        cast("scalar", "a", 0, 1)
-        cast("vector", "a", 1, 0)
-        cast("scalar", "a", 1, 1)
-        quantise("a", 0)
-        quantise("a", 1)
+        cast("scalar", "a", 0, 2)
+        cast("vector", "a", 0, 1)
+        cast("vector", "a", 0, 3)
+        quantise("a", 0, 0, 1)
+        quantise("a", 1, 0, 1)
+        quantise("a", 2, 0, 1)
+        quantise("a", 3, 0, 1)
         pass_t(0, 0, 0, True, False)
-        pass_t(0, 0, 1, False, False)
         pass_t(1, 0, 0, True, False)
-        pass_t(1, 0, 1, False, False)
-        cast("vector", "g", 0, 0)
-        cast("scalar", "g", 0, 1)
-        quantise("g", 0)
+        pass_t(2, 0, 0, True, False)
+        pass_t(3, 0, 0, True, False)
+        cast("vector", "a", 1, 0)
+        cast("scalar", "a", 1, 2)
+        cast("vector", "a", 1, 1)
+        quantise("a", 0, 1, 2)
+        cast("scalar", "a", 1, 3)
+        quantise("a", 1, 1, 2)
+        quantise("a", 2, 1, 2)
+        quantise("a", 3, 1, 2)
+        pass_t(0, 0, 1, False, False)
         pass_q(0, 0, False, True)
+        pass_t(1, 0, 1, False, False)
         pass_q(1, 0, False, True)
-        pass_g(0)
-        pass_g(1)
-        pass_q(2, 0, True, False)
+        pass_t(2, 0, 1, False, False)
+        pass_q(2, 0, False, True)
+        pass_t(3, 0, 1, False, False)
+        pass_q(3, 0, False, True)
         pass_q(0, 1, True, False)
         pass_q(1, 1, True, False)
-        pass_q(2, 1, True, False)
         group_sum(0, 0)
-        cast("scalar", "a", 0, 2)
+        scale_out(0, 0, 0, 512)
         group_sum(1, 0)
-        cast("scalar", "a", 1, 2)
+        scale_out(1, 0, 0, 512)
+        group_sum(2, 0)
+        cast("scalar", "g", 0, 2)
+        cast("vector", "g", 0, 0)
+        cast("vector", "g", 0, 1)
+        pass_q(2, 1, True, False)
+        pass_q(3, 1, True, False)
+        quantise("g", 0, 0, 1)
+        quantise("g", 0, 1, 2)
+        pass_g(0, True)
+        pass_g(1, False)
+        cast("scalar", "g", 0, 3)
+        group_sum(3, 0)
+        passes_t(0, 1)
         add_g(0, 0, 1)
         add_g(1, 0, 1)
-        quantise("a", 2)
+        quantise("g", 1)
         relu(0, 0, 1)
-        scale_out(1, 0, 0, 512)
         relu(1, 0, 1)
+        finish_gpsimd(0, 0, 0, 512)
         finish_gpsimd(1, 0, 0, 512)
-        store(1, 0, 0, 512)
-        passes_t(0, 1)
-        passes_t(2, 0)
         passes_t(1, 1)
+        pass_g(2, True)
+        pass_g(3, False)
         passes_t(2, 1)
-        finish_vector(0, 0, 0, 512)
-        store(0, 0, 0, 512)
-        pass_q(3, 0, True, False)
-        pass_q(3, 1, True, False)
-        cast("scalar", "g", 0, 2)
-        group_sum(0, 1)
-        cast("scalar", "a", 0, 3)
-        group_sum(2, 0)
-        cast("scalar", "a", 1, 3)
-        add_g(0, 1, 2)
-        group_sum(1, 1)
-        quantise("g", 1, 0, 1)
-        pass_g(2)
-        quantise("a", 3)
-        passes_t(3, 0)
         passes_t(3, 1)
-        relu(0, 1, 2)
-        scale_out(0, 1, 0, 512)
-        finish_gpsimd(0, 1, 0, 512)
-        store(0, 1, 0, 512)
-        cast("scalar", "g", 0, 3)
-        add_g(1, 1, 2)
+        group_sum(0, 1)
+        group_sum(1, 1)
         add_g(2, 0, 1)
-        relu(1, 1, 2)
+        add_g(3, 0, 1)
+        store(0, 0, 0, 512)
         relu(2, 0, 1)
-        scale_out(2, 0, 0, 512)
-        group_sum(2, 1)
-        group_sum(3, 0)
-        quantise("g", 1, 1, 2)
-        pass_g(3)
-        finish_gpsimd(2, 0, 0, 512)
+        relu(3, 0, 1)
+        scale_out(0, 1, 0, 512)
+        add_g(0, 1, 2)
+        add_g(1, 1, 2)
+        relu(0, 1, 2)
+        finish_gpsimd(0, 1, 0, 512)
+        relu(1, 1, 2)
+        finish_vector(2, 0, 0, 512)
         store(2, 0, 0, 512)
+        store(1, 0, 0, 512)
+        finish_vector(3, 0, 0, 512)
+        store(3, 0, 0, 512)
+        group_sum(2, 1)
+        group_sum(3, 1)
         add_g(2, 1, 2)
+        add_g(3, 1, 2)
+        store(0, 1, 0, 512)
+        relu(2, 1, 2)
+        relu(3, 1, 2)
         finish_vector(1, 1, 0, 512)
         store(1, 1, 0, 512)
-        relu(2, 1, 2)
-        scale_out(3, 0, 0, 512)
-        group_sum(3, 1)
-        scale_out(3, 1, 0, 512)
         finish_vector(2, 1, 0, 512)
         store(2, 1, 0, 512)
-        add_g(3, 0, 2)
-        finish_fused(3, 0, 0, 512)
-        store(3, 0, 0, 512)
-        finish_fused(3, 1, 0, 512)
+        finish_vector(3, 1, 0, 512)
         store(3, 1, 0, 512)

@@ -18,10 +18,23 @@ ACT = mybir.ActivationFunctionType
 P = 128
 PACK = 4
 K_PASS = P * PACK
-HALF = 512
+TILES = N // P
+HALF = T // 2
 GROUP = T // B
 HALF_GROUPS = HALF // GROUP
-BANK = {(1, 0): 1, (1, 1): 5, (2, 0): 2, (2, 1): 0, (3, 0): 3, (3, 1): 1, (0, 0): 0, (0, 1): 4}
+QUADRANT = 32
+OWN_SHARE = 0.4
+
+XT_FIRST = (4, 8)
+XG_FIRST = 12
+XG_COLS = slice(HALF, HALF + B)
+
+VECTOR_TILES = (0, 1)
+SCALAR_TILES = (2, 3)
+
+GPSIMD_UNITS = ((0, 0), (1, 0), (0, 1))
+
+Z_BANKS = 6
 
 
 def tile_mix_sum_shared_by_neighbours_kernel(
@@ -30,325 +43,234 @@ def tile_mix_sum_shared_by_neighbours_kernel(
     nc = tc.nc
     with ExitStack() as ctx:
         keep = ctx.enter_context(tc.tile_pool(name="keep", bufs=1))
-        zpool = ctx.enter_context(tc.psum_pool(name="zpool", bufs=1))
-        gpool = ctx.enter_context(tc.psum_pool(name="gpool", bufs=2))
+        psum = ctx.enter_context(tc.psum_pool(name="psum", bufs=1))
         ctx.enter_context(tc.manual_schedule())
 
-        def sb(name, shape, dtype):
+        def sbuf(name, shape, dtype):
             return keep.tile(shape, dtype, name=name, align_bytes=64)
 
-        xt_plane = sb("xt_plane", [P, T], U8)
-        wq_plane = sb("wq_plane", [P, N], U8)
-        xq_plane = sb("xq_plane", [P, T], U8)
-        nc.vector.memset(xt_plane[:].bitcast(I32), 0)
-        nc.vector.memset(xq_plane[:].bitcast(I32), 0)
-        nc.vector.memset(wq_plane[:].bitcast(I32), 0)
+        def columns(index, width):
+            return slice(index * width, (index + 1) * width)
 
-        def load_scales(engine, plane, first_row, cols, scales, quads=range(4)):
+        shared_plane = sbuf("shared_plane", [P, T], U8)
+        xq_plane = sbuf("xq_plane", [P, T], U8)
+        wq_plane = sbuf("wq_plane", [P, N], U8)
+        for plane in (shared_plane, xq_plane, wq_plane):
+            nc.vector.memset(plane[:].bitcast(I32), 0)
+
+        def load_bytes(dst, src):
+            nc.sync.dma_start(out=dst.bitcast(I32), in_=src.bitcast(I32))
+
+        def load_scales(plane, first, cols, scales):
             passes = scales.shape[0]
-            for q in quads:
-                rows = slice(32 * q + first_row, 32 * q + first_row + 4 * passes)
-                src = scales[:, 4 * q : 4 * q + 4, :] if passes > 1 else scales[0, 4 * q : 4 * q + 4, :]
-                engine.dma_start(out=plane[rows, cols].bitcast(I32), in_=src.bitcast(I32))
+            for quad in range(P // QUADRANT):
+                rows = slice(QUADRANT * quad + first, QUADRANT * quad + first + 4 * passes)
+                src = scales[:, columns(quad, 4), :] if passes > 1 else scales[0, columns(quad, 4), :]
+                load_bytes(plane[rows, cols], src)
 
+        def load_tokens(h):
+            words = sbuf("xt_words%d" % h, [P, K // K_PASS, HALF], U32)
+            load_bytes(words[:], xt_words.rearrange("z p t r -> p z (t r)")[:, :, columns(h, HALF * PACK)])
+            return words
 
-        raw = {}
+        def load_weight_pass(name, rows):
+            raw = sbuf("raw_" + name, [P, PACK, N], F32)
+            nc.sync.dma_start(out=raw[:], in_=rows.rearrange("(p j) n -> p j n", j=PACK))
+            return raw
 
-        def load_weight(name, w, z, i0, i1):
-            t = sb("raw_%s%d_%d" % (name, z, i0), [P, PACK, (i1 - i0) * P], F32)
-            rows = w[z * K_PASS : (z + 1) * K_PASS, :].rearrange("(p j) n -> p j n", j=PACK)
-            nc.sync.dma_start(out=t[:], in_=rows[:, :, i0 * P : i1 * P])
-            for i in range(i0, i1):
-                raw[name, z, i] = t[:, :, (i - i0) * P : (i - i0 + 1) * P]
+        wq_sb = sbuf("wq_sb", [P, N], U32)
+        xq_sb = sbuf("xq_sb", [P, 2 * T], U8)
+        xg_sb = sbuf("xg_sb", [P, B], U32)
 
-        xt_sb = {}
+        xt_sb, raw = {}, {}
+        xt_sb[0] = load_tokens(0)
+        load_scales(shared_plane, XT_FIRST[0], slice(0, T), xt_scales)
+        raw["wa0"] = load_weight_pass("wa0", wa[columns(0, K_PASS), :])
+        load_scales(xq_plane, 0, slice(0, T), xq_scales)
+        raw["wa1"] = load_weight_pass("wa1", wa[columns(1, K_PASS), :])
+        load_scales(wq_plane, 0, slice(0, N), wq_scales)
+        load_bytes(wq_sb[:], wq_words[0].rearrange("p n r -> p (n r)"))
+        load_bytes(xq_sb[:], xq_words[0])
+        raw["wg"] = load_weight_pass("wg", wg)
+        load_scales(shared_plane, XG_FIRST, XG_COLS, xg_scales)
+        load_bytes(xg_sb[:], xg_words[0].rearrange("p b r -> p (b r)"))
+        xt_sb[1] = load_tokens(1)
 
-        def load_xt(h):
-            t = sb("xt_sb%d" % h, [P, 2, HALF], U32)
-            src = xt_words.rearrange("z p t r -> p z (t r)")[:, :, h * HALF * 4 : (h + 1) * HALF * 4]
-            nc.sync.dma_start(out=t[:].bitcast(I32), in_=src.bitcast(I32))
-            xt_sb[h] = t
+        rounded, codes, planes = {}, {}, {}
 
-        wq_sb = sb("wq_sb", [P, N], U32)
-        xq_sb = sb("xq_sb", [P, 2 * T], U8)
-        xg_sb = sb("xg_sb", [P, B], U32)
-
-        def load_wq():
-            nc.sync.dma_start(out=wq_sb[:].bitcast(I32), in_=wq_words[0].rearrange("p n r -> p (n r)").bitcast(I32))
-
-        def load_xq():
-            nc.sync.dma_start(out=xq_sb[:].bitcast(I32), in_=xq_words[0].bitcast(I32))
-
-        def load_xg():
-            nc.sync.dma_start(out=xg_sb[:].bitcast(I32), in_=xg_words[0].rearrange("p b r -> p (b r)").bitcast(I32))
-
-        def sc_xt(engine, quads):
-            load_scales(engine, xt_plane, 4, slice(0, T), xt_scales, quads)
-
-        def sc_wq(engine, quads):
-            load_scales(engine, wq_plane, 0, slice(0, N), wq_scales, quads)
-
-        def sc_xq(engine, quads):
-            load_scales(engine, xq_plane, 0, slice(0, T), xq_scales, quads)
-
-        def sc_xg(engine, quads):
-            load_scales(engine, xt_plane, 12, slice(HALF, HALF + B), xg_scales, quads)
-
-        sc_xq(nc.gpsimd, (0, 1, 2, 3,))
-        load_weight("a", wa, 0, 0, 4)
-        sc_xt(nc.sync, (0, 1, 2, 3,))
-        load_xt(0)
-        load_weight("a", wa, 1, 0, 4)
-        sc_wq(nc.sync, (0,))
-        load_wq()
-        load_xq()
-        sc_wq(nc.sync, (1, 2, 3,))
-        load_weight("g", wg, 0, 0, 4)
-        load_xg()
-        sc_xg(nc.sync, (0, 1, 2, 3,))
-        load_xt(1)
-
-        staged, codes, planes = {}, {}, {}
-        for name, count in (("a", 4), ("g", 2)):
-            for i in range(count):
-                staged[name, i] = sb("staged_%s%d" % (name, i), [P, 2 * K_PASS], BF16)
-                codes[name, i] = sb("codes_%s%d" % (name, i), [P, 2 * P], U32)
-                planes[name, i] = sb("planes_%s%d" % (name, i), [P, 2 * P], U8)
-
-        def cast(engine, name, z, i):
-            key, slot = ((name, i), z) if name == "a" else ((name, i // 2), i % 2)
-            dst = staged[key][:, slot * K_PASS : (slot + 1) * K_PASS]
-            src = raw[name, z, i]
-            if engine == "gpsimd":
-                nc.gpsimd.tensor_scalar(
-                    out=dst.rearrange("p (c j) -> p c j", j=PACK),
-                    in0=src.rearrange("p j c -> p c j"),
-                    scalar1=1.0,
-                    scalar2=0.0,
-                    op0=ALU.mult,
-                    op1=ALU.add,
-                )
-                return
-            dst = dst.rearrange("p (c u j) -> p c j u", u=4, j=PACK)
-            src = src.rearrange("p j (c u) -> p c j u", u=4)
-            if engine == "vector":
+        def round_weights(name, i):
+            rounded[name, i] = sbuf("rounded_%s_%d" % (name, i), [P, K_PASS], BF16)
+            dst = rounded[name, i][:].rearrange("p (c u j) -> p c j u", u=4, j=PACK)
+            src = raw[name][:, :, columns(i, P)].rearrange("p j (c u) -> p c j u", u=4)
+            if i in VECTOR_TILES:
                 nc.vector.tensor_copy(out=dst, in_=src)
             else:
                 nc.scalar.copy(out=dst, in_=src)
 
-        def quantise(name, i, z0=0, z1=2):
+        def quantise(name, i):
+            codes[name, i] = sbuf("codes_%s_%d" % (name, i), [P, P], U32)
+            planes[name, i] = sbuf("plane_%s_%d" % (name, i), [P, P], U8)
             nc.vector.quantize_mx(
-                out=codes[name, i][:, z0 * P : z1 * P].bitcast(FP8X4),
-                scales=planes[name, i][:, z0 * P : z1 * P],
-                in_=staged[name, i][:, z0 * K_PASS : z1 * K_PASS],
-            )
-        zb, gb = {}, {}
-
-        def z_tile(i, h):
-            if (i, h) not in zb:
-                zb[i, h] = zpool.tile([P, HALF], F32, name="z%d%d" % (i, h), tag="bank%d" % BANK[i, h])
-            return zb[i, h]
-
-        def pass_q(i, h, start, stop):
-            nc.tensor.matmul_mx(
-                out=z_tile(i, h)[:],
-                lhsT=wq_sb[:, i * P : (i + 1) * P].bitcast(FP8X4),
-                lhsT_scale=wq_plane[:, i * P : (i + 1) * P],
-                rhs=xq_sb[:, 2 * h * HALF : 2 * (h + 1) * HALF].bitcast(FP4X4),
-                rhs_scale=xq_plane[:, h * HALF : (h + 1) * HALF],
-                start=start,
-                stop=stop,
+                out=codes[name, i][:].bitcast(FP8X4), scales=planes[name, i][:], in_=rounded[name, i][:]
             )
 
-        def pass_t(i, h, z, start, stop):
+        z_bank, g_bank = {}, {}
+
+        def open_unit(i, h):
+            z_bank[i, h] = psum.tile([P, HALF], F32, name="z%d_%d" % (i, h), tag="z%d" % (len(z_bank) % Z_BANKS))
+
+        def pass_xt(i, h, z, start=False, stop=False):
+            name = "wa%d" % z
             nc.tensor.matmul_mx(
-                out=z_tile(i, h)[:],
-                lhsT=codes["a", i][:, z * P : (z + 1) * P].bitcast(FP8X4),
-                lhsT_scale=planes["a", i][:, z * P : (z + 1) * P],
+                out=z_bank[i, h][:],
+                lhsT=codes[name, i][:].bitcast(FP8X4),
+                lhsT_scale=planes[name, i][:],
                 rhs=xt_sb[h][:, z, :].bitcast(FP8X4),
-                rhs_scale=xt_plane[4 + 4 * z :, h * HALF : (h + 1) * HALF],
+                rhs_scale=shared_plane[XT_FIRST[z] :, columns(h, HALF)],
                 start=start,
                 stop=stop,
             )
 
-        def passes_t(i, h):
-            pass_t(i, h, 0, False, False)
-            pass_t(i, h, 1, False, True)
-
-        def pass_g(i, fresh):
-            if fresh:
-                gb[i // 2] = gpool.tile([P, 2 * B], F32, name="g")
-            slot = slice((i % 2) * P, (i % 2 + 1) * P)
+        def pass_xq(i, h, start=False, stop=False):
             nc.tensor.matmul_mx(
-                out=gb[i // 2][:, (i % 2) * B : (i % 2 + 1) * B],
-                lhsT=codes["g", i // 2][:, slot].bitcast(FP8X4),
-                lhsT_scale=planes["g", i // 2][:, slot],
-                rhs=xg_sb[:].bitcast(FP8X4),
-                rhs_scale=xt_plane[12:, HALF : HALF + B],
-                start=True,
-                stop=True,
+                out=z_bank[i, h][:],
+                lhsT=wq_sb[:, columns(i, P)].bitcast(FP8X4),
+                lhsT_scale=wq_plane[:, columns(i, P)],
+                rhs=xq_sb[:, columns(h, 2 * HALF)].bitcast(FP4X4),
+                rhs_scale=xq_plane[:, columns(h, HALF)],
+                start=start,
+                stop=stop,
             )
 
-        sums, pre, shared, scaled, res = {}, {}, {}, {}, {}
-        for i in range(4):
-            sums[i] = sb("sums%d" % i, [P, B], F32)
-            pre[i] = sb("pre%d" % i, [P, B], F32)
-            shared[i] = sb("shared%d" % i, [P, B], F32)
+        def passes_g(pair):
+            bank = psum.tile([P, len(pair) * B], F32, name="g%d" % pair[0])
+            for slot, i in enumerate(pair):
+                g_bank[i] = bank[:, columns(slot, B)]
+                nc.tensor.matmul_mx(
+                    out=g_bank[i],
+                    lhsT=codes["wg", i][:].bitcast(FP8X4),
+                    lhsT_scale=planes["wg", i][:],
+                    rhs=xg_sb[:].bitcast(FP8X4),
+                    rhs_scale=shared_plane[XG_FIRST:, XG_COLS],
+                    start=True,
+                    stop=True,
+                )
 
-        def groups(h0, h1):
-            return slice(h0 * HALF_GROUPS, h1 * HALF_GROUPS)
+        sums, before_relu, shared, own, result = {}, {}, {}, {}, {}
 
-        def group_sum(i, h):
+        def by_group(ap):
+            return ap.rearrange("p (b j) -> p b j", j=GROUP)
+
+        def sum_groups(i, h):
+            sums[i, h] = sbuf("sums%d_%d" % (i, h), [P, HALF_GROUPS], F32)
             nc.vector.tensor_reduce(
-                out=sums[i][:, groups(h, h + 1)],
-                in_=zb[i, h][:].rearrange("p (b j) -> p b j", j=GROUP),
-                axis=mybir.AxisListType.X,
-                op=ALU.add,
+                out=sums[i, h][:], in_=by_group(z_bank[i, h][:]), axis=mybir.AxisListType.X, op=ALU.add
             )
 
-        def add_g(i, h0, h1):
+        def add_g(i, h):
+            before_relu[i, h] = sbuf("before_relu%d_%d" % (i, h), [P, HALF_GROUPS], F32)
             nc.vector.scalar_tensor_tensor(
-                out=pre[i][:, groups(h0, h1)],
-                in0=sums[i][:, groups(h0, h1)],
+                out=before_relu[i, h][:],
+                in0=sums[i, h][:],
                 scalar=1.0 / GROUP,
-                in1=gb[i // 2][:, (i % 2) * B : (i % 2 + 1) * B][:, groups(h0, h1)],
+                in1=g_bank[i][:, columns(h, HALF_GROUPS)],
                 op0=ALU.mult,
                 op1=ALU.add,
             )
 
-        def relu(i, h0, h1):
-            nc.scalar.activation(out=shared[i][:, groups(h0, h1)], in_=pre[i][:, groups(h0, h1)], func=ACT.Relu)
+        def relu(i, h):
+            shared[i, h] = sbuf("shared%d_%d" % (i, h), [P, HALF_GROUPS], F32)
+            nc.scalar.activation(out=shared[i, h][:], in_=before_relu[i, h][:], func=ACT.Relu)
 
-        def spread(i, h, c0, c1):
-            b0, b1 = h * HALF_GROUPS + c0 // GROUP, h * HALF_GROUPS + c1 // GROUP
-            return shared[i][:, b0:b1].unsqueeze(2).to_broadcast([P, b1 - b0, GROUP])
+        def copy_own(i, h):
+            own[i, h] = sbuf("own%d_%d" % (i, h), [P, HALF], F32)
+            nc.scalar.activation(out=own[i, h][:], in_=z_bank[i, h][:], func=ACT.Copy, scale=OWN_SHARE)
 
-        def store(i, h, c0, c1):
-            nc.sync.dma_start(out=out[i * P : (i + 1) * P, h * HALF + c0 : h * HALF + c1], in_=res[i, h, c0][:])
+        def finish(i, h):
+            result[i, h] = sbuf("result%d_%d" % (i, h), [P, HALF], F32)
+            repeated = shared[i, h][:].unsqueeze(2).to_broadcast([P, HALF_GROUPS, GROUP])
+            if (i, h) in GPSIMD_UNITS:
+                nc.gpsimd.tensor_tensor(
+                    out=by_group(result[i, h][:]), in0=by_group(own[i, h][:]), in1=repeated, op=ALU.add
+                )
+            else:
+                nc.vector.scalar_tensor_tensor(
+                    out=by_group(result[i, h][:]),
+                    in0=by_group(z_bank[i, h][:]),
+                    scalar=OWN_SHARE,
+                    in1=repeated,
+                    op0=ALU.mult,
+                    op1=ALU.add,
+                )
 
-        def finish_vector(i, h, c0=0, c1=HALF):
-            res[i, h, c0] = sb("res%d_%d_%d" % (i, h, c0), [P, c1 - c0], F32)
-            nc.vector.scalar_tensor_tensor(
-                out=res[i, h, c0][:].rearrange("p (b j) -> p b j", j=GROUP),
-                in0=zb[i, h][:, c0:c1].rearrange("p (b j) -> p b j", j=GROUP),
-                scalar=0.4,
-                in1=spread(i, h, c0, c1),
-                op0=ALU.mult,
-                op1=ALU.add,
-            )
+        def store(i, h):
+            nc.sync.dma_start(out=out[columns(i, P), columns(h, HALF)], in_=result[i, h][:])
 
-        def finish_fused(i, h, c0=0, c1=HALF):
-            res[i, h, c0] = sb("res%d_%d_%d" % (i, h, c0), [P, c1 - c0], F32)
-            b0, b1 = h * HALF_GROUPS + c0 // GROUP, h * HALF_GROUPS + c1 // GROUP
-            nc.vector.scalar_tensor_tensor(
-                out=res[i, h, c0][:].rearrange("p (b j) -> p b j", j=GROUP),
-                in0=pre[i][:, b0:b1].unsqueeze(2).to_broadcast([P, b1 - b0, GROUP]),
-                scalar=0.0,
-                in1=scaled[i, h, c0][:].rearrange("p (b j) -> p b j", j=GROUP),
-                op0=ALU.max,
-                op1=ALU.add,
-            )
+        for z in range(K // K_PASS):
+            for i in range(TILES):
+                round_weights("wa%d" % z, i)
+            for i in range(TILES):
+                quantise("wa%d" % z, i)
+        for i in range(TILES):
+            open_unit(i, 0)
+            pass_xt(i, 0, 0, start=True)
+        for i in range(TILES):
+            pass_xt(i, 0, 1)
+            pass_xq(i, 0, stop=True)
 
-        def scale_out(i, h, c0=0, c1=HALF):
-            scaled[i, h, c0] = sb("scaled%d_%d_%d" % (i, h, c0), [P, c1 - c0], F32)
-            nc.scalar.activation(out=scaled[i, h, c0][:], in_=zb[i, h][:, c0:c1], func=ACT.Copy, scale=0.4)
+        for i in VECTOR_TILES:
+            sum_groups(i, 0)
+            copy_own(i, 0)
+        sum_groups(2, 0)
+        for i in range(TILES):
+            open_unit(i, 1)
+            pass_xq(i, 1, start=True)
 
-        def finish_gpsimd(i, h, c0=0, c1=HALF):
-            res[i, h, c0] = sb("res%d_%d_%d" % (i, h, c0), [P, c1 - c0], F32)
-            nc.gpsimd.tensor_tensor(
-                out=res[i, h, c0][:].rearrange("p (b j) -> p b j", j=GROUP),
-                in0=scaled[i, h, c0][:].rearrange("p (b j) -> p b j", j=GROUP),
-                in1=spread(i, h, c0, c1),
-                op=ALU.add,
-            )
+        for i in range(TILES):
+            round_weights("wg", i)
+        for i in VECTOR_TILES:
+            quantise("wg", i)
+        passes_g(VECTOR_TILES)
+        sum_groups(3, 0)
+        for i in VECTOR_TILES:
+            add_g(i, 0)
+            relu(i, 0)
+        for i in SCALAR_TILES:
+            quantise("wg", i)
+        for i in VECTOR_TILES:
+            finish(i, 0)
 
-        cast("vector", "a", 0, 0)
-        cast("scalar", "a", 0, 2)
-        cast("vector", "a", 0, 1)
-        cast("vector", "a", 0, 3)
-        quantise("a", 0, 0, 1)
-        quantise("a", 1, 0, 1)
-        quantise("a", 2, 0, 1)
-        quantise("a", 3, 0, 1)
-        pass_t(0, 0, 0, True, False)
-        pass_t(1, 0, 0, True, False)
-        pass_t(2, 0, 0, True, False)
-        pass_t(3, 0, 0, True, False)
-        cast("vector", "a", 1, 0)
-        cast("scalar", "a", 1, 2)
-        cast("vector", "a", 1, 1)
-        quantise("a", 0, 1, 2)
-        cast("scalar", "a", 1, 3)
-        quantise("a", 1, 1, 2)
-        quantise("a", 2, 1, 2)
-        quantise("a", 3, 1, 2)
-        pass_t(0, 0, 1, False, False)
-        pass_q(0, 0, False, True)
-        pass_t(1, 0, 1, False, False)
-        pass_q(1, 0, False, True)
-        pass_t(2, 0, 1, False, False)
-        pass_q(2, 0, False, True)
-        pass_t(3, 0, 1, False, False)
-        pass_q(3, 0, False, True)
-        pass_q(0, 1, True, False)
-        pass_q(1, 1, True, False)
-        group_sum(0, 0)
-        scale_out(0, 0, 0, 512)
-        group_sum(1, 0)
-        scale_out(1, 0, 0, 512)
-        group_sum(2, 0)
-        cast("scalar", "g", 0, 2)
-        cast("vector", "g", 0, 0)
-        cast("vector", "g", 0, 1)
-        pass_q(2, 1, True, False)
-        pass_q(3, 1, True, False)
-        quantise("g", 0, 0, 1)
-        quantise("g", 0, 1, 2)
-        pass_g(0, True)
-        pass_g(1, False)
-        cast("scalar", "g", 0, 3)
-        group_sum(3, 0)
-        passes_t(0, 1)
-        add_g(0, 0, 1)
-        add_g(1, 0, 1)
-        quantise("g", 1)
-        relu(0, 0, 1)
-        relu(1, 0, 1)
-        finish_gpsimd(0, 0, 0, 512)
-        finish_gpsimd(1, 0, 0, 512)
-        passes_t(1, 1)
-        pass_g(2, True)
-        pass_g(3, False)
-        passes_t(2, 1)
-        passes_t(3, 1)
-        group_sum(0, 1)
-        group_sum(1, 1)
-        add_g(2, 0, 1)
-        add_g(3, 0, 1)
-        store(0, 0, 0, 512)
-        relu(2, 0, 1)
-        relu(3, 0, 1)
-        scale_out(0, 1, 0, 512)
-        add_g(0, 1, 2)
-        add_g(1, 1, 2)
-        relu(0, 1, 2)
-        finish_gpsimd(0, 1, 0, 512)
-        relu(1, 1, 2)
-        finish_vector(2, 0, 0, 512)
-        store(2, 0, 0, 512)
-        store(1, 0, 0, 512)
-        finish_vector(3, 0, 0, 512)
-        store(3, 0, 0, 512)
-        group_sum(2, 1)
-        group_sum(3, 1)
-        add_g(2, 1, 2)
-        add_g(3, 1, 2)
-        store(0, 1, 0, 512)
-        relu(2, 1, 2)
-        relu(3, 1, 2)
-        finish_vector(1, 1, 0, 512)
-        store(1, 1, 0, 512)
-        finish_vector(2, 1, 0, 512)
-        store(2, 1, 0, 512)
-        finish_vector(3, 1, 0, 512)
-        store(3, 1, 0, 512)
+        def close_units(pair):
+            for i in pair:
+                pass_xt(i, 1, 0)
+                pass_xt(i, 1, 1, stop=True)
+
+        close_units(VECTOR_TILES)
+        passes_g(SCALAR_TILES)
+        close_units(SCALAR_TILES)
+
+        for i in VECTOR_TILES:
+            sum_groups(i, 1)
+        for i in SCALAR_TILES:
+            add_g(i, 0)
+            relu(i, 0)
+        copy_own(0, 1)
+        for i in VECTOR_TILES:
+            add_g(i, 1)
+            relu(i, 1)
+        finish(0, 1)
+        for i in SCALAR_TILES:
+            finish(i, 0)
+        for i in SCALAR_TILES:
+            sum_groups(i, 1)
+        for i in SCALAR_TILES:
+            add_g(i, 1)
+            relu(i, 1)
+        for i in range(1, TILES):
+            finish(i, 1)
+
+        for pair in zip(VECTOR_TILES, SCALAR_TILES):
+            for i in pair:
+                store(i, 0)
+        for i in range(TILES):
+            store(i, 1)

@@ -23,11 +23,11 @@ HALF = T // 2
 GROUP = T // B
 HALF_GROUPS = HALF // GROUP
 QUADRANT = 32
+SCALE_ROWS = 4
 OWN_SHARE = 0.4
 
-XT_FIRST = (4, 8)
-XG_FIRST = 12
-XG_COLS = slice(HALF, HALF + B)
+XT_FIRST = 4
+XG_FIRST = 8
 
 VECTOR_TILES = (0, 1)
 SCALAR_TILES = (2, 3)
@@ -52,21 +52,20 @@ def tile_mix_sum_shared_by_neighbours_kernel(
         def columns(index, width):
             return slice(index * width, (index + 1) * width)
 
-        shared_plane = sbuf("shared_plane", [P, T], U8)
-        xq_plane = sbuf("xq_plane", [P, T], U8)
-        wq_plane = sbuf("wq_plane", [P, N], U8)
-        for plane in (shared_plane, xq_plane, wq_plane):
+        xt_plane = sbuf("xt_plane", [P, K // K_PASS, T], U8)
+        xq_plane = sbuf("xq_plane", [P, 1, T], U8)
+        wq_plane = sbuf("wq_plane", [P, 1, N], U8)
+        xg_plane = sbuf("xg_plane", [P, 1, B], U8)
+        for plane in (xt_plane, xq_plane, wq_plane, xg_plane):
             nc.vector.memset(plane[:].bitcast(I32), 0)
 
         def load_bytes(dst, src):
             nc.sync.dma_start(out=dst.bitcast(I32), in_=src.bitcast(I32))
 
-        def load_scales(plane, first, cols, scales):
-            passes = scales.shape[0]
-            for quad in range(P // QUADRANT):
-                rows = slice(QUADRANT * quad + first, QUADRANT * quad + first + 4 * passes)
-                src = scales[:, columns(quad, 4), :] if passes > 1 else scales[0, columns(quad, 4), :]
-                load_bytes(plane[rows, cols], src)
+        def load_scales(plane, first, scales):
+            by_row = scales.rearrange("z (quad r) c -> r quad z c", r=SCALE_ROWS)
+            for r in range(SCALE_ROWS):
+                load_bytes(plane[first + r : P : QUADRANT], by_row[r])
 
         def load_tokens(h):
             words = sbuf("xt_words%d" % h, [P, K // K_PASS, HALF], U32)
@@ -84,15 +83,15 @@ def tile_mix_sum_shared_by_neighbours_kernel(
 
         xt_sb, raw = {}, {}
         xt_sb[0] = load_tokens(0)
-        load_scales(shared_plane, XT_FIRST[0], slice(0, T), xt_scales)
+        load_scales(xt_plane, XT_FIRST, xt_scales)
         raw["wa0"] = load_weight_pass("wa0", wa[columns(0, K_PASS), :])
-        load_scales(xq_plane, 0, slice(0, T), xq_scales)
+        load_scales(xq_plane, 0, xq_scales)
         raw["wa1"] = load_weight_pass("wa1", wa[columns(1, K_PASS), :])
-        load_scales(wq_plane, 0, slice(0, N), wq_scales)
+        load_scales(wq_plane, 0, wq_scales)
         load_bytes(wq_sb[:], wq_words[0].rearrange("p n r -> p (n r)"))
         load_bytes(xq_sb[:], xq_words[0])
         raw["wg"] = load_weight_pass("wg", wg)
-        load_scales(shared_plane, XG_FIRST, XG_COLS, xg_scales)
+        load_scales(xg_plane, XG_FIRST, xg_scales)
         load_bytes(xg_sb[:], xg_words[0].rearrange("p b r -> p (b r)"))
         xt_sb[1] = load_tokens(1)
 
@@ -126,7 +125,7 @@ def tile_mix_sum_shared_by_neighbours_kernel(
                 lhsT=codes[name, i][:].bitcast(FP8X4),
                 lhsT_scale=planes[name, i][:],
                 rhs=xt_sb[h][:, z, :].bitcast(FP8X4),
-                rhs_scale=shared_plane[XT_FIRST[z] :, columns(h, HALF)],
+                rhs_scale=xt_plane[XT_FIRST:, z, columns(h, HALF)],
                 start=start,
                 stop=stop,
             )
@@ -135,9 +134,9 @@ def tile_mix_sum_shared_by_neighbours_kernel(
             nc.tensor.matmul_mx(
                 out=z_bank[i, h][:],
                 lhsT=wq_sb[:, columns(i, P)].bitcast(FP8X4),
-                lhsT_scale=wq_plane[:, columns(i, P)],
+                lhsT_scale=wq_plane[:, 0, columns(i, P)],
                 rhs=xq_sb[:, columns(h, 2 * HALF)].bitcast(FP4X4),
-                rhs_scale=xq_plane[:, columns(h, HALF)],
+                rhs_scale=xq_plane[:, 0, columns(h, HALF)],
                 start=start,
                 stop=stop,
             )
@@ -151,7 +150,7 @@ def tile_mix_sum_shared_by_neighbours_kernel(
                     lhsT=codes["wg", i][:].bitcast(FP8X4),
                     lhsT_scale=planes["wg", i][:],
                     rhs=xg_sb[:].bitcast(FP8X4),
-                    rhs_scale=shared_plane[XG_FIRST:, XG_COLS],
+                    rhs_scale=xg_plane[XG_FIRST:, 0, :],
                     start=True,
                     stop=True,
                 )
@@ -218,25 +217,25 @@ def tile_mix_sum_shared_by_neighbours_kernel(
             pass_xt(i, 0, 1)
             pass_xq(i, 0, stop=True)
 
-        for i in VECTOR_TILES:
+        for i in range(TILES - 1):
             sum_groups(i, 0)
-            copy_own(i, 0)
-        sum_groups(2, 0)
-        for i in range(TILES):
+        copy_own(0, 0)
+        for i in range(TILES - 1):
             open_unit(i, 1)
             pass_xq(i, 1, start=True)
 
         for i in range(TILES):
             round_weights("wg", i)
+        copy_own(1, 0)
         for i in VECTOR_TILES:
             quantise("wg", i)
         passes_g(VECTOR_TILES)
-        sum_groups(3, 0)
+        sum_groups(TILES - 1, 0)
+        for i in SCALAR_TILES:
+            quantise("wg", i)
         for i in VECTOR_TILES:
             add_g(i, 0)
             relu(i, 0)
-        for i in SCALAR_TILES:
-            quantise("wg", i)
         for i in VECTOR_TILES:
             finish(i, 0)
 
@@ -247,6 +246,8 @@ def tile_mix_sum_shared_by_neighbours_kernel(
 
         close_units(VECTOR_TILES)
         passes_g(SCALAR_TILES)
+        open_unit(TILES - 1, 1)
+        pass_xq(TILES - 1, 1, start=True)
         close_units(SCALAR_TILES)
 
         for i in VECTOR_TILES:

from contextlib import ExitStack

import concourse.mybir as mybir

K, L, M, T, B, N = 1024, 512, 512, 1024, 256, 512
FLOPS = 2 * N * (K * T + L * T + M * B)

F32 = mybir.dt.float32
BF16 = mybir.dt.bfloat16
I32 = mybir.dt.int32
U32 = mybir.dt.uint32
U8 = mybir.dt.uint8
FP8X4 = mybir.dt.float8_e4m3fn_x4
FP4X4 = mybir.dt.float4_e2m1fn_x4
ALU = mybir.AluOpType
ACT = mybir.ActivationFunctionType

P = 128
PACK = 4
K_PASS = P * PACK
TILES = N // P
HALF = T // 2
GROUP = T // B
HALF_GROUPS = HALF // GROUP
QUADRANT = 32
SCALE_ROWS = 4
OWN_SHARE = 0.4

XT_FIRST = 4
XG_FIRST = 8

VECTOR_TILES = (0, 1)
SCALAR_TILES = (2, 3)

GPSIMD_UNITS = ((0, 0), (1, 0), (0, 1))

Z_BANKS = 6


def tile_mix_sum_shared_by_neighbours_kernel(
    tc, xt_words, xt_scales, wa, xq_words, xq_scales, wq_words, wq_scales, xg_words, xg_scales, wg, out
):
    nc = tc.nc
    with ExitStack() as ctx:
        keep = ctx.enter_context(tc.tile_pool(name="keep", bufs=1))
        psum = ctx.enter_context(tc.psum_pool(name="psum", bufs=1))
        ctx.enter_context(tc.manual_schedule())

        def sbuf(name, shape, dtype):
            return keep.tile(shape, dtype, name=name, align_bytes=64)

        def columns(index, width):
            return slice(index * width, (index + 1) * width)

        xt_plane = sbuf("xt_plane", [P, K // K_PASS, T], U8)
        xq_plane = sbuf("xq_plane", [P, 1, T], U8)
        wq_plane = sbuf("wq_plane", [P, 1, N], U8)
        xg_plane = sbuf("xg_plane", [P, 1, B], U8)
        for plane in (xt_plane, xq_plane, wq_plane, xg_plane):
            nc.vector.memset(plane[:].bitcast(I32), 0)

        def load_bytes(dst, src):
            nc.sync.dma_start(out=dst.bitcast(I32), in_=src.bitcast(I32))

        def load_scales(plane, first, scales):
            by_row = scales.rearrange("z (quad r) c -> r quad z c", r=SCALE_ROWS)
            for r in range(SCALE_ROWS):
                load_bytes(plane[first + r : P : QUADRANT], by_row[r])

        def load_tokens(h):
            words = sbuf("xt_words%d" % h, [P, K // K_PASS, HALF], U32)
            load_bytes(words[:], xt_words.rearrange("z p t r -> p z (t r)")[:, :, columns(h, HALF * PACK)])
            return words

        def load_weight_pass(name, rows):
            raw = sbuf("raw_" + name, [P, PACK, N], F32)
            nc.sync.dma_start(out=raw[:], in_=rows.rearrange("(p j) n -> p j n", j=PACK))
            return raw

        wq_sb = sbuf("wq_sb", [P, N], U32)
        xq_sb = sbuf("xq_sb", [P, 2 * T], U8)
        xg_sb = sbuf("xg_sb", [P, B], U32)

        xt_sb, raw = {}, {}
        xt_sb[0] = load_tokens(0)
        load_scales(xt_plane, XT_FIRST, xt_scales)
        raw["wa0"] = load_weight_pass("wa0", wa[columns(0, K_PASS), :])
        load_scales(xq_plane, 0, xq_scales)
        raw["wa1"] = load_weight_pass("wa1", wa[columns(1, K_PASS), :])
        load_scales(wq_plane, 0, wq_scales)
        load_bytes(wq_sb[:], wq_words[0].rearrange("p n r -> p (n r)"))
        load_bytes(xq_sb[:], xq_words[0])
        raw["wg"] = load_weight_pass("wg", wg)
        load_scales(xg_plane, XG_FIRST, xg_scales)
        load_bytes(xg_sb[:], xg_words[0].rearrange("p b r -> p (b r)"))
        xt_sb[1] = load_tokens(1)

        rounded, codes, planes = {}, {}, {}

        def round_weights(name, i):
            rounded[name, i] = sbuf("rounded_%s_%d" % (name, i), [P, K_PASS], BF16)
            dst = rounded[name, i][:].rearrange("p (c u j) -> p c j u", u=4, j=PACK)
            src = raw[name][:, :, columns(i, P)].rearrange("p j (c u) -> p c j u", u=4)
            if i in VECTOR_TILES:
                nc.vector.tensor_copy(out=dst, in_=src)
            else:
                nc.scalar.copy(out=dst, in_=src)

        def quantise(name, i):
            codes[name, i] = sbuf("codes_%s_%d" % (name, i), [P, P], U32)
            planes[name, i] = sbuf("plane_%s_%d" % (name, i), [P, P], U8)
            nc.vector.quantize_mx(
                out=codes[name, i][:].bitcast(FP8X4), scales=planes[name, i][:], in_=rounded[name, i][:]
            )

        z_bank, g_bank = {}, {}

        def open_unit(i, h):
            z_bank[i, h] = psum.tile([P, HALF], F32, name="z%d_%d" % (i, h), tag="z%d" % (len(z_bank) % Z_BANKS))

        def pass_xt(i, h, z, start=False, stop=False):
            name = "wa%d" % z
            nc.tensor.matmul_mx(
                out=z_bank[i, h][:],
                lhsT=codes[name, i][:].bitcast(FP8X4),
                lhsT_scale=planes[name, i][:],
                rhs=xt_sb[h][:, z, :].bitcast(FP8X4),
                rhs_scale=xt_plane[XT_FIRST:, z, columns(h, HALF)],
                start=start,
                stop=stop,
            )

        def pass_xq(i, h, start=False, stop=False):
            nc.tensor.matmul_mx(
                out=z_bank[i, h][:],
                lhsT=wq_sb[:, columns(i, P)].bitcast(FP8X4),
                lhsT_scale=wq_plane[:, 0, columns(i, P)],
                rhs=xq_sb[:, columns(h, 2 * HALF)].bitcast(FP4X4),
                rhs_scale=xq_plane[:, 0, columns(h, HALF)],
                start=start,
                stop=stop,
            )

        def passes_g(pair):
            bank = psum.tile([P, len(pair) * B], F32, name="g%d" % pair[0])
            for slot, i in enumerate(pair):
                g_bank[i] = bank[:, columns(slot, B)]
                nc.tensor.matmul_mx(
                    out=g_bank[i],
                    lhsT=codes["wg", i][:].bitcast(FP8X4),
                    lhsT_scale=planes["wg", i][:],
                    rhs=xg_sb[:].bitcast(FP8X4),
                    rhs_scale=xg_plane[XG_FIRST:, 0, :],
                    start=True,
                    stop=True,
                )

        sums, before_relu, shared, own, result = {}, {}, {}, {}, {}

        def by_group(ap):
            return ap.rearrange("p (b j) -> p b j", j=GROUP)

        def sum_groups(i, h):
            sums[i, h] = sbuf("sums%d_%d" % (i, h), [P, HALF_GROUPS], F32)
            nc.vector.tensor_reduce(
                out=sums[i, h][:], in_=by_group(z_bank[i, h][:]), axis=mybir.AxisListType.X, op=ALU.add
            )

        def add_g(i, h):
            before_relu[i, h] = sbuf("before_relu%d_%d" % (i, h), [P, HALF_GROUPS], F32)
            nc.vector.scalar_tensor_tensor(
                out=before_relu[i, h][:],
                in0=sums[i, h][:],
                scalar=1.0 / GROUP,
                in1=g_bank[i][:, columns(h, HALF_GROUPS)],
                op0=ALU.mult,
                op1=ALU.add,
            )

        def relu(i, h):
            shared[i, h] = sbuf("shared%d_%d" % (i, h), [P, HALF_GROUPS], F32)
            nc.scalar.activation(out=shared[i, h][:], in_=before_relu[i, h][:], func=ACT.Relu)

        def copy_own(i, h):
            own[i, h] = sbuf("own%d_%d" % (i, h), [P, HALF], F32)
            nc.scalar.activation(out=own[i, h][:], in_=z_bank[i, h][:], func=ACT.Copy, scale=OWN_SHARE)

        def finish(i, h):
            result[i, h] = sbuf("result%d_%d" % (i, h), [P, HALF], F32)
            repeated = shared[i, h][:].unsqueeze(2).to_broadcast([P, HALF_GROUPS, GROUP])
            if (i, h) in GPSIMD_UNITS:
                nc.gpsimd.tensor_tensor(
                    out=by_group(result[i, h][:]), in0=by_group(own[i, h][:]), in1=repeated, op=ALU.add
                )
            else:
                nc.vector.scalar_tensor_tensor(
                    out=by_group(result[i, h][:]),
                    in0=by_group(z_bank[i, h][:]),
                    scalar=OWN_SHARE,
                    in1=repeated,
                    op0=ALU.mult,
                    op1=ALU.add,
                )

        def store(i, h):
            nc.sync.dma_start(out=out[columns(i, P), columns(h, HALF)], in_=result[i, h][:])

        for z in range(K // K_PASS):
            for i in range(TILES):
                round_weights("wa%d" % z, i)
            for i in range(TILES):
                quantise("wa%d" % z, i)
        for i in range(TILES):
            open_unit(i, 0)
            pass_xt(i, 0, 0, start=True)
        for i in range(TILES):
            pass_xt(i, 0, 1)
            pass_xq(i, 0, stop=True)

        for i in range(TILES - 1):
            sum_groups(i, 0)
        copy_own(0, 0)
        for i in range(TILES - 1):
            open_unit(i, 1)
            pass_xq(i, 1, start=True)

        for i in range(TILES):
            round_weights("wg", i)
        copy_own(1, 0)
        for i in VECTOR_TILES:
            quantise("wg", i)
        passes_g(VECTOR_TILES)
        sum_groups(TILES - 1, 0)
        for i in SCALAR_TILES:
            quantise("wg", i)
        for i in VECTOR_TILES:
            add_g(i, 0)
            relu(i, 0)
        for i in VECTOR_TILES:
            finish(i, 0)

        def close_units(pair):
            for i in pair:
                pass_xt(i, 1, 0)
                pass_xt(i, 1, 1, stop=True)

        close_units(VECTOR_TILES)
        passes_g(SCALAR_TILES)
        open_unit(TILES - 1, 1)
        pass_xq(TILES - 1, 1, start=True)
        close_units(SCALAR_TILES)

        for i in VECTOR_TILES:
            sum_groups(i, 1)
        for i in SCALAR_TILES:
            add_g(i, 0)
            relu(i, 0)
        copy_own(0, 1)
        for i in VECTOR_TILES:
            add_g(i, 1)
            relu(i, 1)
        finish(0, 1)
        for i in SCALAR_TILES:
            finish(i, 0)
        for i in SCALAR_TILES:
            sum_groups(i, 1)
        for i in SCALAR_TILES:
            add_g(i, 1)
            relu(i, 1)
        for i in range(1, TILES):
            finish(i, 1)

        for pair in zip(VECTOR_TILES, SCALAR_TILES):
            for i in pair:
                store(i, 0)
        for i in range(TILES):
            store(i, 1)
